import numpy as np
import ml_dtypes


def mxq(x, axis, fmt="e4m3"):
    dtype, down = {"e4m3": (ml_dtypes.float8_e4m3fn, 7), "e5m2": (ml_dtypes.float8_e5m2, 14)}[fmt]
    v = np.moveaxis(np.asarray(x, np.float32).astype(ml_dtypes.bfloat16).astype(np.float64), axis, -1)
    blocks = v.reshape(v.shape[:-1] + (-1, 32))
    amax = np.abs(blocks).max(-1, keepdims=True)
    byte = np.maximum(np.where(amax > 0, np.frexp(amax)[1] - 1 + 127, 0) - down, 1)
    scale = np.exp2(byte - 127.0)
    codes = (blocks / scale).astype(np.float32).astype(dtype).astype(np.float64)
    return np.moveaxis((codes * scale).reshape(v.shape), -1, axis)


WIDE = False


def mx_kscale(k):
    if not WIDE:
        return np.ones(k)
    levels = np.array([10, -10, 5, -5, 0])
    if k % 512:
        return np.exp2(np.random.permutation(np.resize(levels, k // 32))).repeat(32)
    a = np.empty((k // 512, 16))
    for p in range(k // 512):
        a[p, :8] = np.random.permutation(np.resize(levels, 8))
        for g in range(8):
            far = levels[np.abs(levels - a[p, g]) >= 10]
            a[p, g + 8] = far[np.random.randint(len(far))]
    return np.exp2(a.ravel()).repeat(32)


BF16 = ml_dtypes.bfloat16


def bf(x):
    return np.asarray(x, np.float32).astype(BF16)


def f64(x):
    return np.asarray(x).astype(np.float64)


B, K, C = 2048, 1024, 512


def draw0():
    s = mx_kscale(K)
    t = mx_kscale(B)
    unit = t[:, None] * s
    return {"u": bf(np.random.standard_normal((B, K)) * unit),
            "h": bf(0.8 * np.random.standard_normal((K, K)) / np.sqrt(K) / s[:, None] * s),
            "lo": bf(-(0.6 + 0.9 * np.random.random((B, K))) * unit),
            "hi": bf((0.6 + 0.9 * np.random.random((B, K))) * unit),
            "psi": bf(np.random.standard_normal((B, C)) / np.sqrt(B) / t[:, None])}


def core(u, h, lo, hi, psi):
    u = f64(u)
    g = mxq(u, 1, "e4m3") @ mxq(f64(h), 0, "e4m3")
    v = np.minimum(np.maximum(u - g, f64(lo)), f64(hi))
    c = mxq(f64(psi), 0, "e4m3").T @ mxq(v, 0, "e4m3")
    return c


def e4m3fn_bytes(y):
    return np.clip(np.asarray(y, np.float64), -448.0, 448.0).astype(np.float32).astype(ml_dtypes.float8_e4m3fn).view(np.uint8)


def e4m3fn_values(b):
    return np.asarray(b, np.uint8).view(ml_dtypes.float8_e4m3fn).astype(np.float64)


def setup_inputs():
    d = draw0()
    x0 = np.asarray(d['psi']).astype(np.float64)
    s = (np.max(np.abs(x0), axis=(1,), keepdims=True) / 448.0).astype(np.float32)
    out = {}
    for k, v in d.items():
        if k == 'psi':
            out['psi_bytes'] = e4m3fn_bytes(x0 / s.astype(np.float64))
            out['psi_scale'] = s
        else:
            out[k] = v
    return out


def reference(u, h, lo, hi, psi_bytes, psi_scale):
    return core(u, h, lo, hi, e4m3fn_values(psi_bytes) * psi_scale.astype(np.float64))

@@ -1,0 +1,435 @@
+from contextlib import ExitStack
+
+import concourse.mybir as mybir
+from concourse.masks import make_identity
+
+B, K, C = 2048, 1024, 512
+FLOPS = 2 * B * K * K + 2 * B * K * C
+
+F32 = mybir.dt.float32
+BF16 = mybir.dt.bfloat16
+U32 = mybir.dt.uint32
+U8 = mybir.dt.uint8
+FP8 = mybir.dt.float8_e4m3fn
+FP8X4 = mybir.dt.float8_e4m3fn_x4
+ALU = mybir.AluOpType
+COPY = mybir.ActivationFunctionType.Copy
+
+P = 128
+PACK = 4
+GROUP = P * PACK
+HALF = 512
+QUARTER = HALF // 2
+H_VECTOR = 320
+
+G_BANKS = ("bank0", "bank1", "bank2", "bank3")
+V_BANKS = ("bank4", "bank5")
+T_BANKS = ("bank6", "bank7")
+
+UNITS = ((0, 0), (1, 0), (0, 1), (1, 1), (2, 0), (3, 0), (2, 1), (3, 1))
+
+
+def tile_mpc_box_step_s7_kernel(tc, u, h, lo, hi, psi_bytes, psi_scale, out):
+    nc = tc.nc
+    with ExitStack() as ctx:
+        keep = ctx.enter_context(tc.tile_pool(name="keep", bufs=1))
+        work = ctx.enter_context(tc.tile_pool(name="work", bufs=2))
+        psum = ctx.enter_context(tc.psum_pool(name="psum", bufs=1))
+        ctx.enter_context(tc.manual_schedule())
+
+        ident_f32 = keep.tile([P, P], F32, name="ident_f32")
+        make_identity(nc, ident_f32[:])
+        ident_bf = keep.tile([P, P], BF16, name="ident_bf")
+        make_identity(nc, ident_bf[:])
+
+        u_sb, lo_sb, hi_sb, h_raw, bytes_sb = {}, {}, {}, {}, {}
+        h_codes, h_scales, u_codes, u_scales = {}, {}, {}, {}
+        v_codes, v_scales, psi_codes, psi_scales = {}, {}, {}, {}
+
+        def rows(x, g):
+            return x[g * GROUP : (g + 1) * GROUP, :].rearrange("(p t) n -> p t n", t=PACK)
+
+        def alloc_u(g):
+            u_sb[g] = work.tile([P, PACK, K], BF16, name="u%d" % g, tag="u", bufs=3)
+
+        def load_u(g, t0, t1):
+            nc.sync.dma_start(out=u_sb[g][:, t0:t1, :], in_=rows(u, g)[:, t0:t1, :])
+
+        def load_box(g, n):
+            cols = slice(n * HALF, (n + 1) * HALF)
+            lo_sb[g, n] = work.tile([P, PACK, HALF], BF16, name="lo%d%d" % (g, n), tag="lo", bufs=6)
+            nc.sync.dma_start(out=lo_sb[g, n][:], in_=rows(lo, g)[:, :, cols])
+            hi_sb[g, n] = work.tile([P, PACK, HALF], BF16, name="hi%d%d" % (g, n), tag="hi", bufs=6)
+            nc.sync.dma_start(out=hi_sb[g, n][:], in_=rows(hi, g)[:, :, cols])
+
+        def load_h(k, n):
+            h_raw[k, n] = work.tile([P, PACK, HALF], BF16, name="h%d%d" % (k, n), tag="h_raw", bufs=4)
+            nc.sync.dma_start(out=h_raw[k, n][:], in_=rows(h, k)[:, :, n * HALF : (n + 1) * HALF])
+
+        def load_psi(g):
+            bytes_sb[g] = keep.tile([P, PACK * C], U8, name="bytes%d" % g)
+            nc.sync.dma_start(
+                out=bytes_sb[g][:],
+                in_=psi_bytes[g * GROUP : (g + 1) * GROUP, :].rearrange("(p t) c -> p (t c)", t=PACK),
+            )
+
+        def quantize(name, pool_codes, pool_scales, key, grouped, words):
+            pool_codes[key] = keep.tile([P, words], U32, name="c_" + name, align_bytes=64)
+            pool_scales[key] = keep.tile([P, words], U8, name="s_" + name, align_bytes=64)
+            nc.vector.quantize_mx(
+                out=pool_codes[key][:].bitcast(FP8X4), scales=pool_scales[key][:], in_=grouped
+            )
+
+        def interleave(engine_copy, dst, src, c0, c1):
+            engine_copy(out=dst[:, c0:c1, :], in_=src[:, :, c0:c1].rearrange("p t n -> p n t"))
+
+        def interleave_pe(bank, src, q):
+            half = P
+            ps = psum.tile([P, QUARTER, PACK], BF16, name="il_" + bank, tag=bank)
+            for s in range(QUARTER // half):
+                c0 = q * QUARTER + s * half
+                nc.tensor.matmul(
+                    out=ps[:, s * half : (s + 1) * half, :],
+                    lhsT=ident_bf[:],
+                    rhs=src[:, :, c0 : c0 + half].rearrange("p t n -> p n t"),
+                    start=True,
+                    stop=True,
+                )
+            return ps
+
+        def grouped_tile(name):
+            return work.tile([P, HALF, PACK], BF16, name=name, tag="grouped", bufs=3, align_bytes=64)
+
+        def flat(t):
+            return t[:].rearrange("p n t -> p (n t)")
+
+        xt = {}
+        ut = {}
+
+        def transpose_u(j, bank):
+            g, t = divmod(j, PACK)
+            words = u_sb[g][:, t, :].bitcast(F32)
+            xt[j] = psum.tile([P, 2, 2, P], F32, name="xt%d" % j, tag=bank)
+            for k in range(2):
+                for w in range(2):
+                    nc.tensor.transpose(
+                        xt[j][:, k, w, :],
+                        words[:, 256 * k + w : 256 * (k + 1) : 2],
+                        ident_f32[:],
+                    )
+
+        def copy_ut(j):
+            ut[j] = work.tile([P, 2, P, 2], F32, name="ut%d" % j, tag="ut", bufs=4, align_bytes=64)
+            nc.scalar.copy(out=ut[j][:], in_=xt[j][:].rearrange("p k w r -> p k r w"))
+
+        def quantize_u(j):
+            grouped = ut[j][:].rearrange("p k r w -> p (k r w)").bitcast(BF16)
+            quantize("u%d" % j, u_codes, u_scales, j, grouped, 2 * P)
+
+        g_ps = {}
+
+        def stage1(i, t):
+            g, n = UNITS[i]
+            j = g * PACK + t
+            g_ps[i, t] = psum.tile([P, HALF], F32, name="g%d%d" % (i, t), tag=G_BANKS[t])
+            for k in range(2):
+                nc.tensor.matmul_mx(
+                    out=g_ps[i, t][:],
+                    lhsT=u_codes[j][:, k * P : (k + 1) * P].bitcast(FP8X4),
+                    lhsT_scale=u_scales[j][:, k * P : (k + 1) * P],
+                    rhs=h_codes[k, n][:].bitcast(FP8X4),
+                    rhs_scale=h_scales[k, n][:],
+                    start=(k == 0),
+                    stop=(k == 1),
+                )
+
+        d_sb, m_sb, v_sb, vp, vg = {}, {}, {}, {}, {}
+
+        def sub(i, t):
+            g, n = UNITS[i]
+            if t == 0:
+                d_sb[i] = work.tile([P, PACK, HALF], BF16, name="d%d" % i, tag="d", bufs=2)
+            nc.vector.tensor_tensor(
+                out=d_sb[i][:, t, :],
+                in0=u_sb[g][:, t, n * HALF : (n + 1) * HALF],
+                in1=g_ps[i, t][:],
+                op=ALU.subtract,
+            )
+
+        def clamp_lo(i, q):
+            if q == 0:
+                m_sb[i] = work.tile([P, PACK, HALF], BF16, name="m%d" % i, tag="m", bufs=2)
+            cols = slice(q * QUARTER, (q + 1) * QUARTER)
+            nc.vector.tensor_tensor(
+                out=m_sb[i][:, :, cols], in0=d_sb[i][:, :, cols], in1=lo_sb[UNITS[i]][:, :, cols], op=ALU.max
+            )
+
+        def clamp_hi(i, q):
+            if q == 0:
+                v_sb[i] = work.tile([P, PACK, HALF], BF16, name="v%d" % i, tag="v", bufs=2)
+            cols = slice(q * QUARTER, (q + 1) * QUARTER)
+            nc.vector.tensor_tensor(
+                out=v_sb[i][:, :, cols], in0=m_sb[i][:, :, cols], in1=hi_sb[UNITS[i]][:, :, cols], op=ALU.min
+            )
+
+        def v_interleave(i, q):
+            vp[i, q] = interleave_pe(V_BANKS[q], v_sb[i], q)
+
+        def v_copy(i, q):
+            if q == 0:
+                vg[i] = work.tile([P, HALF, PACK], BF16, name="vg%d" % i, tag="vg", bufs=2, align_bytes=64)
+            nc.scalar.copy(out=vg[i][:, q * QUARTER : (q + 1) * QUARTER, :], in_=vp[i, q][:])
+
+        def quantize_v(i):
+            quantize("v%d" % i, v_codes, v_scales, UNITS[i], flat(vg[i]), HALF)
+
+        planes, pg = {}, {}
+
+        def psi_widen(g):
+            planes[g] = work.tile([P, PACK, C], BF16, name="planes%d" % g, tag="planes", bufs=2)
+            for t in range(PACK):
+                nc.scalar.activation(
+                    out=planes[g][:, t, :],
+                    in_=bytes_sb[g][:, t * C : (t + 1) * C].bitcast(FP8),
+                    func=COPY,
+                    scale=scale_sb[:, g, t : t + 1],
+                )
+
+        def psi_interleave(g):
+            pg[g] = grouped_tile("pg%d" % g)
+            interleave(nc.scalar.copy, pg[g], planes[g], 0, QUARTER)
+            interleave(nc.scalar.copy, pg[g], planes[g], QUARTER, HALF)
+
+        def quantize_psi(g):
+            quantize("psi%d" % g, psi_codes, psi_scales, g, flat(pg[g]), C)
+
+        acc = {}
+
+        def stage2_open(n, c, bank):
+            acc[n, c] = psum.tile([P, HALF], F32, name="acc%d%d" % (n, c), tag=bank)
+
+        def stage2(n, c, groups):
+            for g in groups:
+                nc.tensor.matmul_mx(
+                    out=acc[n, c][:],
+                    lhsT=psi_codes[g][:, c * P : (c + 1) * P].bitcast(FP8X4),
+                    lhsT_scale=psi_scales[g][:, c * P : (c + 1) * P],
+                    rhs=v_codes[g, n][:].bitcast(FP8X4),
+                    rhs_scale=v_scales[g, n][:],
+                    start=(g == 0),
+                    stop=(g == 3),
+                )
+
+        def store(n, c, engine_copy):
+            res = work.tile([P, HALF], F32, name="res%d%d" % (n, c), tag="res", bufs=4)
+            engine_copy(out=res[:], in_=acc[n, c][:])
+            nc.sync.dma_start(out=out[c * P : (c + 1) * P, n * HALF : (n + 1) * HALF], in_=res[:])
+
+        alloc_u(0)
+        load_u(0, 0, 1)
+        load_h(0, 0)
+        load_h(1, 0)
+        for t in range(1, PACK):
+            load_u(0, t, t + 1)
+        load_box(0, 0)
+        alloc_u(1)
+        for t in range(PACK):
+            load_u(1, t, t + 1)
+        load_box(1, 0)
+        load_h(0, 1)
+        load_h(1, 1)
+        scale_sb = keep.tile([P, 4, PACK], F32, name="scale_sb")
+        nc.sync.dma_start(
+            out=scale_sb[:], in_=psi_scale.rearrange("(g p t) o -> p g (t o)", g=4, p=P, t=PACK)
+        )
+        load_psi(0)
+        load_box(0, 1)
+        load_box(1, 1)
+        alloc_u(2)
+        load_u(2, 0, PACK)
+        load_psi(1)
+        load_box(2, 0)
+        load_psi(2)
+        load_psi(3)
+
+        hg = {}
+        hg[0] = grouped_tile("hg00")
+        hg[1] = grouped_tile("hg10")
+        transpose_u(0, T_BANKS[0])
+        copy_ut(0)
+        interleave(nc.vector.tensor_copy, hg[0], h_raw[0, 0], 0, H_VECTOR)
+        interleave(nc.scalar.copy, hg[0], h_raw[0, 0], H_VECTOR, HALF)
+        quantize_u(0)
+        interleave(nc.vector.tensor_copy, hg[1], h_raw[1, 0], 0, H_VECTOR)
+        interleave(nc.scalar.copy, hg[1], h_raw[1, 0], H_VECTOR, HALF)
+        transpose_u(1, T_BANKS[1])
+        copy_ut(1)
+        quantize("h00", h_codes, h_scales, (0, 0), flat(hg[0]), HALF)
+        transpose_u(2, V_BANKS[0])
+        copy_ut(2)
+        quantize("h10", h_codes, h_scales, (1, 0), flat(hg[1]), HALF)
+        transpose_u(3, V_BANKS[1])
+        copy_ut(3)
+        stage1(0, 0)
+        quantize_u(1)
+        stage1(0, 1)
+        quantize_u(2)
+        stage1(0, 2)
+
+        sub(0, 0)
+        quantize_u(3)
+        stage1(0, 3)
+        sub(0, 1)
+        sub(0, 2)
+        transpose_u(4, T_BANKS[0])
+        copy_ut(4)
+        transpose_u(5, T_BANKS[1])
+        copy_ut(5)
+        sub(0, 3)
+        clamp_lo(0, 0)
+        clamp_lo(0, 1)
+        quantize_u(4)
+        transpose_u(6, T_BANKS[0])
+        copy_ut(6)
+        transpose_u(7, T_BANKS[1])
+        copy_ut(7)
+        clamp_hi(0, 0)
+        stage1(1, 0)
+        v_interleave(0, 0)
+        v_copy(0, 0)
+        quantize_u(5)
+        clamp_hi(0, 1)
+        v_interleave(0, 1)
+        v_copy(0, 1)
+        stage1(1, 1)
+        quantize_u(6)
+        quantize_u(7)
+        stage1(1, 2)
+        stage1(1, 3)
+
+        for t in range(PACK):
+            sub(1, t)
+        hg[2] = grouped_tile("hg01")
+        interleave(nc.scalar.copy, hg[2], h_raw[0, 1], 0, QUARTER)
+        interleave(nc.scalar.copy, hg[2], h_raw[0, 1], QUARTER, HALF)
+        hg[3] = grouped_tile("hg11")
+        for q in range(2):
+            ps = interleave_pe(T_BANKS[q], h_raw[1, 1], q)
+            nc.scalar.copy(out=hg[3][:, q * QUARTER : (q + 1) * QUARTER, :], in_=ps[:])
+        quantize_v(0)
+        clamp_lo(1, 0)
+        clamp_lo(1, 1)
+        quantize("h01", h_codes, h_scales, (0, 1), flat(hg[2]), HALF)
+        clamp_hi(1, 0)
+        v_interleave(1, 0)
+        v_copy(1, 0)
+        quantize("h11", h_codes, h_scales, (1, 1), flat(hg[3]), HALF)
+        clamp_hi(1, 1)
+        stage1(2, 0)
+        stage1(2, 1)
+        v_interleave(1, 1)
+        v_copy(1, 1)
+        stage1(2, 2)
+        stage1(2, 3)
+
+        def body(i, tiles=(), psi_q=None, psi_w=None, psi_i=None, before=None, after_q=None):
+            if tiles:
+                transpose_u(tiles[0], T_BANKS[0])
+                copy_ut(tiles[0])
+                transpose_u(tiles[1], T_BANKS[1])
+                copy_ut(tiles[1])
+            for t in range(PACK):
+                sub(i, t)
+            if psi_w is not None:
+                psi_widen(psi_w)
+            if i < 7:
+                for t in range(PACK):
+                    stage1(i + 1, t)
+            if tiles:
+                transpose_u(tiles[2], T_BANKS[0])
+                copy_ut(tiles[2])
+                transpose_u(tiles[3], T_BANKS[1])
+                copy_ut(tiles[3])
+            if before is not None:
+                before()
+            if psi_i is not None:
+                psi_interleave(psi_i)
+            quantize_v(i - 1)
+            clamp_lo(i, 0)
+            clamp_lo(i, 1)
+            if psi_q is not None:
+                quantize_psi(psi_q)
+            if tiles:
+                quantize_u(tiles[0])
+            if after_q is not None:
+                after_q()
+            clamp_hi(i, 0)
+            v_interleave(i, 0)
+            v_copy(i, 0)
+            if tiles:
+                quantize_u(tiles[1])
+            clamp_hi(i, 1)
+            v_interleave(i, 1)
+            v_copy(i, 1)
+            if tiles:
+                quantize_u(tiles[2])
+                quantize_u(tiles[3])
+
+        body(2, tiles=(8, 9, 10, 11), psi_w=0)
+        alloc_u(3)
+        load_u(3, 0, PACK)
+        load_box(3, 0)
+        body(3, tiles=(12, 13, 14, 15), psi_i=0)
+        load_box(2, 1)
+        load_box(3, 1)
+        body(4, psi_q=0, psi_w=1, psi_i=1)
+
+        def open_half0():
+            stage2_open(0, 0, T_BANKS[0])
+            stage2_open(0, 1, T_BANKS[1])
+            stage2(0, 0, (0, 1))
+            stage2(0, 1, (0, 1))
+
+        body(5, psi_q=1, psi_w=2, psi_i=2, after_q=open_half0)
+
+        def close_half0_first():
+            stage2(0, 0, (2,))
+            stage2(0, 1, (2,))
+
+        def close_half0():
+            quantize_psi(3)
+            stage2(0, 0, (3,))
+            store(0, 0, nc.scalar.copy)
+            stage2(0, 1, (3,))
+            store(0, 1, nc.scalar.copy)
+
+        body(6, psi_q=2, psi_w=3, psi_i=3, after_q=close_half0_first)
+
+        for t in range(PACK):
+            sub(7, t)
+        close_half0()
+        stage2_open(0, 2, T_BANKS[0])
+        stage2_open(0, 3, T_BANKS[1])
+        stage2(0, 2, (0, 1, 2, 3))
+        stage2(0, 3, (0, 1, 2, 3))
+        quantize_v(6)
+        clamp_lo(7, 0)
+        clamp_lo(7, 1)
+        for c in range(4):
+            stage2_open(1, c, G_BANKS[c])
+        for c in range(4):
+            stage2(1, c, (0, 1))
+        store(0, 2, nc.scalar.copy)
+        store(0, 3, nc.scalar.copy)
+        clamp_hi(7, 0)
+        v_interleave(7, 0)
+        v_copy(7, 0)
+        clamp_hi(7, 1)
+        v_interleave(7, 1)
+        v_copy(7, 1)
+        for c in range(4):
+            stage2(1, c, (2,))
+        quantize_v(7)
+        for c in range(4):
+            stage2(1, c, (3,))
+            store(1, c, nc.scalar.copy if c % 2 == 0 else nc.vector.tensor_copy)

@@ -83,11 +83,11 @@ def tile_mpc_box_step_s7_kernel(tc, u, h, lo, hi, psi_bytes, psi_scale, out):
         def interleave(engine_copy, dst, src, c0, c1):
             engine_copy(out=dst[:, c0:c1, :], in_=src[:, :, c0:c1].rearrange("p t n -> p n t"))
 
-        def interleave_pe(bank, src, q):
+        def interleave_pe(bank, src, first):
             half = P
             ps = psum.tile([P, QUARTER, PACK], BF16, name="il_" + bank, tag=bank)
             for s in range(QUARTER // half):
-                c0 = q * QUARTER + s * half
+                c0 = first + s * half
                 nc.tensor.matmul(
                     out=ps[:, s * half : (s + 1) * half, :],
                     lhsT=ident_bf[:],
@@ -148,37 +148,40 @@ def tile_mpc_box_step_s7_kernel(tc, u, h, lo, hi, psi_bytes, psi_scale, out):
         def sub(i, t):
             g, n = UNITS[i]
             if t == 0:
-                d_sb[i] = work.tile([P, PACK, HALF], BF16, name="d%d" % i, tag="d", bufs=2)
+                d_sb[i] = work.tile([P, 2, PACK, QUARTER], BF16, name="d%d" % i, tag="d", bufs=2)
             nc.vector.tensor_tensor(
-                out=d_sb[i][:, t, :],
-                in0=u_sb[g][:, t, n * HALF : (n + 1) * HALF],
-                in1=g_ps[i, t][:],
+                out=d_sb[i][:, :, t, :],
+                in0=u_sb[g][:, t, n * HALF : (n + 1) * HALF].rearrange("p (q n) -> p q n", q=2),
+                in1=g_ps[i, t][:].rearrange("p (q n) -> p q n", q=2),
                 op=ALU.subtract,
             )
 
         def clamp_lo(i, q):
             if q == 0:
-                m_sb[i] = work.tile([P, PACK, HALF], BF16, name="m%d" % i, tag="m", bufs=2)
+                m_sb[i] = work.tile([P, 2, PACK, QUARTER], BF16, name="m%d" % i, tag="m", bufs=2)
             cols = slice(q * QUARTER, (q + 1) * QUARTER)
             nc.vector.tensor_tensor(
-                out=m_sb[i][:, :, cols], in0=d_sb[i][:, :, cols], in1=lo_sb[UNITS[i]][:, :, cols], op=ALU.max
+                out=m_sb[i][:, q, :, :], in0=d_sb[i][:, q, :, :], in1=lo_sb[UNITS[i]][:, :, cols], op=ALU.max
             )
 
         def clamp_hi(i, q):
-            if q == 0:
-                v_sb[i] = work.tile([P, PACK, HALF], BF16, name="v%d" % i, tag="v", bufs=2)
+            v_sb[i, q] = work.tile([P, PACK, QUARTER], BF16, name="v%d%d" % (i, q), tag="v", bufs=4)
             cols = slice(q * QUARTER, (q + 1) * QUARTER)
             nc.vector.tensor_tensor(
-                out=v_sb[i][:, :, cols], in0=m_sb[i][:, :, cols], in1=hi_sb[UNITS[i]][:, :, cols], op=ALU.min
+                out=v_sb[i, q][:], in0=m_sb[i][:, q, :, :], in1=hi_sb[UNITS[i]][:, :, cols], op=ALU.min
             )
 
-        def v_interleave(i, q):
-            vp[i, q] = interleave_pe(V_BANKS[q], v_sb[i], q)
-
-        def v_copy(i, q):
+        def v_tile(i, q):
             if q == 0:
                 vg[i] = work.tile([P, HALF, PACK], BF16, name="vg%d" % i, tag="vg", bufs=2, align_bytes=64)
-            nc.scalar.copy(out=vg[i][:, q * QUARTER : (q + 1) * QUARTER, :], in_=vp[i, q][:])
+            return vg[i][:, q * QUARTER : (q + 1) * QUARTER, :]
+
+        def v_interleave(i, q):
+            vp[i, q] = interleave_pe(V_BANKS[q], v_sb[i, q], 0)
+            nc.scalar.copy(out=v_tile(i, q), in_=vp[i, q][:])
+
+        def v_direct(i, q, engine_copy):
+            engine_copy(out=v_tile(i, q), in_=v_sb[i, q][:].rearrange("p t n -> p n t"))
 
         def quantize_v(i):
             quantize("v%d" % i, v_codes, v_scales, UNITS[i], flat(vg[i]), HALF)
@@ -199,6 +202,12 @@ def tile_mpc_box_step_s7_kernel(tc, u, h, lo, hi, psi_bytes, psi_scale, out):
             pg[g] = grouped_tile("pg%d" % g)
             interleave(nc.scalar.copy, pg[g], planes[g], 0, QUARTER)
             interleave(nc.scalar.copy, pg[g], planes[g], QUARTER, HALF)
+
+        def psi_interleave_pe(g):
+            pg[g] = grouped_tile("pg%d" % g)
+            for q in range(2):
+                ps = interleave_pe(V_BANKS[q], planes[g], q * QUARTER)
+                nc.scalar.copy(out=pg[g][:, q * QUARTER : (q + 1) * QUARTER, :], in_=ps[:])
 
         def quantize_psi(g):
             quantize("psi%d" % g, psi_codes, psi_scales, g, flat(pg[g]), C)
@@ -231,25 +240,25 @@ def tile_mpc_box_step_s7_kernel(tc, u, h, lo, hi, psi_bytes, psi_scale, out):
         load_h(1, 0)
         for t in range(1, PACK):
             load_u(0, t, t + 1)
-        load_box(0, 0)
-        alloc_u(1)
-        for t in range(PACK):
-            load_u(1, t, t + 1)
-        load_box(1, 0)
-        load_h(0, 1)
-        load_h(1, 1)
         scale_sb = keep.tile([P, 4, PACK], F32, name="scale_sb")
         nc.sync.dma_start(
             out=scale_sb[:], in_=psi_scale.rearrange("(g p t) o -> p g (t o)", g=4, p=P, t=PACK)
         )
         load_psi(0)
+        load_box(0, 0)
+        alloc_u(1)
+        for t in range(PACK):
+            load_u(1, t, t + 1)
+        load_h(0, 1)
+        load_h(1, 1)
+        load_box(1, 0)
         load_box(0, 1)
-        load_box(1, 1)
+        load_psi(1)
         alloc_u(2)
         load_u(2, 0, PACK)
-        load_psi(1)
-        load_box(2, 0)
+        load_box(1, 1)
         load_psi(2)
+        load_box(2, 0)
         load_psi(3)
 
         hg = {}
@@ -275,158 +284,141 @@ def tile_mpc_box_step_s7_kernel(tc, u, h, lo, hi, psi_bytes, psi_scale, out):
         stage1(0, 1)
         quantize_u(2)
         stage1(0, 2)
+        psi_widen(0)
 
         sub(0, 0)
         quantize_u(3)
         stage1(0, 3)
         sub(0, 1)
         sub(0, 2)
-        transpose_u(4, T_BANKS[0])
-        copy_ut(4)
-        transpose_u(5, T_BANKS[1])
-        copy_ut(5)
+        for s, j in enumerate((4, 5, 6, 7)):
+            transpose_u(j, T_BANKS[s % 2])
+            copy_ut(j)
         sub(0, 3)
         clamp_lo(0, 0)
         clamp_lo(0, 1)
         quantize_u(4)
-        transpose_u(6, T_BANKS[0])
-        copy_ut(6)
-        transpose_u(7, T_BANKS[1])
-        copy_ut(7)
-        clamp_hi(0, 0)
         stage1(1, 0)
+        clamp_hi(0, 0)
         v_interleave(0, 0)
-        v_copy(0, 0)
         quantize_u(5)
+        stage1(1, 1)
         clamp_hi(0, 1)
         v_interleave(0, 1)
-        v_copy(0, 1)
-        stage1(1, 1)
         quantize_u(6)
-        quantize_u(7)
         stage1(1, 2)
+        quantize_u(7)
         stage1(1, 3)
-
-        for t in range(PACK):
-            sub(1, t)
         hg[2] = grouped_tile("hg01")
         interleave(nc.scalar.copy, hg[2], h_raw[0, 1], 0, QUARTER)
         interleave(nc.scalar.copy, hg[2], h_raw[0, 1], QUARTER, HALF)
         hg[3] = grouped_tile("hg11")
         for q in range(2):
-            ps = interleave_pe(T_BANKS[q], h_raw[1, 1], q)
+            ps = interleave_pe(T_BANKS[q], h_raw[1, 1], q * QUARTER)
             nc.scalar.copy(out=hg[3][:, q * QUARTER : (q + 1) * QUARTER, :], in_=ps[:])
-        quantize_v(0)
-        clamp_lo(1, 0)
-        clamp_lo(1, 1)
-        quantize("h01", h_codes, h_scales, (0, 1), flat(hg[2]), HALF)
-        clamp_hi(1, 0)
-        v_interleave(1, 0)
-        v_copy(1, 0)
-        quantize("h11", h_codes, h_scales, (1, 1), flat(hg[3]), HALF)
-        clamp_hi(1, 1)
-        stage1(2, 0)
-        stage1(2, 1)
-        v_interleave(1, 1)
-        v_copy(1, 1)
-        stage1(2, 2)
-        stage1(2, 3)
 
-        def body(i, tiles=(), psi_q=None, psi_w=None, psi_i=None, before=None, after_q=None):
-            if tiles:
-                transpose_u(tiles[0], T_BANKS[0])
-                copy_ut(tiles[0])
-                transpose_u(tiles[1], T_BANKS[1])
-                copy_ut(tiles[1])
+        def nothing():
+            return None
+
+        def body(i, tiles=(), scalar_work=nothing, early_q=nothing, mid_q=nothing, late_q=nothing, pe_work=nothing, pe_mid=nothing, pe_late=nothing):
+            for s, j in enumerate(tiles):
+                transpose_u(j, T_BANKS[s % 2])
+                copy_ut(j)
             for t in range(PACK):
                 sub(i, t)
-            if psi_w is not None:
-                psi_widen(psi_w)
-            if i < 7:
+            early_q()
+            if i not in (1, 7):
                 for t in range(PACK):
                     stage1(i + 1, t)
-            if tiles:
-                transpose_u(tiles[2], T_BANKS[0])
-                copy_ut(tiles[2])
-                transpose_u(tiles[3], T_BANKS[1])
-                copy_ut(tiles[3])
-            if before is not None:
-                before()
-            if psi_i is not None:
-                psi_interleave(psi_i)
-            quantize_v(i - 1)
+            pe_work()
+            scalar_work()
             clamp_lo(i, 0)
             clamp_lo(i, 1)
-            if psi_q is not None:
-                quantize_psi(psi_q)
-            if tiles:
-                quantize_u(tiles[0])
-            if after_q is not None:
-                after_q()
+            if i == 1:
+                quantize("h01", h_codes, h_scales, (0, 1), flat(hg[2]), HALF)
+            quantize_v(i - 1)
+            if i == 1:
+                quantize("h11", h_codes, h_scales, (1, 1), flat(hg[3]), HALF)
+                for t in range(PACK):
+                    stage1(i + 1, t)
+            pe_mid()
             clamp_hi(i, 0)
-            v_interleave(i, 0)
-            v_copy(i, 0)
-            if tiles:
-                quantize_u(tiles[1])
+            if i < 6:
+                v_interleave(i, 0)
+            else:
+                v_direct(i, 0, nc.scalar.copy)
+            mid_q()
             clamp_hi(i, 1)
-            v_interleave(i, 1)
-            v_copy(i, 1)
-            if tiles:
-                quantize_u(tiles[2])
-                quantize_u(tiles[3])
+            if i < 6:
+                v_interleave(i, 1)
+            else:
+                v_direct(i, 1, nc.scalar.copy)
+            pe_late()
+            late_q()
 
-        body(2, tiles=(8, 9, 10, 11), psi_w=0)
+        body(1, scalar_work=lambda: psi_interleave(0))
+        body(
+            2,
+            tiles=(8, 9, 10, 11),
+            scalar_work=lambda: psi_widen(1),
+            early_q=lambda: quantize_psi(0),
+            mid_q=lambda: quantize_u(8),
+            late_q=lambda: [quantize_u(j) for j in (9, 10, 11)],
+        )
         alloc_u(3)
         load_u(3, 0, PACK)
         load_box(3, 0)
-        body(3, tiles=(12, 13, 14, 15), psi_i=0)
+        body(
+            3,
+            tiles=(12, 13, 14, 15),
+            scalar_work=lambda: psi_interleave(1),
+            early_q=lambda: quantize_u(12),
+            mid_q=lambda: quantize_u(13),
+            late_q=lambda: [quantize_u(j) for j in (14, 15)],
+        )
         load_box(2, 1)
         load_box(3, 1)
-        body(4, psi_q=0, psi_w=1, psi_i=1)
 
-        def open_half0():
-            stage2_open(0, 0, T_BANKS[0])
-            stage2_open(0, 1, T_BANKS[1])
-            stage2(0, 0, (0, 1))
-            stage2(0, 1, (0, 1))
+        def psi_work(g):
+            psi_widen(g)
+            psi_interleave_pe(g)
 
-        body(5, psi_q=1, psi_w=2, psi_i=2, after_q=open_half0)
+        body(4, early_q=lambda: quantize_psi(1), scalar_work=lambda: psi_work(2))
 
-        def close_half0_first():
-            stage2(0, 0, (2,))
-            stage2(0, 1, (2,))
+        def half0_first():
+            for c in range(2):
+                stage2_open(0, c, T_BANKS[c])
+                stage2(0, c, (0, 1))
 
-        def close_half0():
-            quantize_psi(3)
-            stage2(0, 0, (3,))
-            store(0, 0, nc.scalar.copy)
-            stage2(0, 1, (3,))
-            store(0, 1, nc.scalar.copy)
+        body(5, early_q=lambda: quantize_psi(2), scalar_work=lambda: psi_work(3), pe_work=half0_first)
 
-        body(6, psi_q=2, psi_w=3, psi_i=3, after_q=close_half0_first)
+        def half0_close():
+            for c in range(2):
+                stage2(0, c, (2, 3))
+                store(0, c, nc.scalar.copy)
+
+        def half0_second():
+            for c in range(2, 4):
+                stage2_open(0, c, T_BANKS[c - 2])
+                stage2(0, c, (0, 1))
+
+        body(6, early_q=lambda: quantize_psi(3), pe_mid=half0_close, pe_late=half0_second)
 
         for t in range(PACK):
             sub(7, t)
-        close_half0()
-        stage2_open(0, 2, T_BANKS[0])
-        stage2_open(0, 3, T_BANKS[1])
-        stage2(0, 2, (0, 1, 2, 3))
-        stage2(0, 3, (0, 1, 2, 3))
-        quantize_v(6)
-        clamp_lo(7, 0)
-        clamp_lo(7, 1)
+        for c in range(2, 4):
+            stage2(0, c, (2, 3))
+            store(0, c, nc.scalar.copy)
         for c in range(4):
             stage2_open(1, c, G_BANKS[c])
-        for c in range(4):
             stage2(1, c, (0, 1))
-        store(0, 2, nc.scalar.copy)
-        store(0, 3, nc.scalar.copy)
+        clamp_lo(7, 0)
+        clamp_lo(7, 1)
+        quantize_v(6)
         clamp_hi(7, 0)
-        v_interleave(7, 0)
-        v_copy(7, 0)
+        v_direct(7, 0, nc.scalar.copy)
         clamp_hi(7, 1)
-        v_interleave(7, 1)
-        v_copy(7, 1)
+        v_direct(7, 1, nc.vector.tensor_copy)
         for c in range(4):
             stage2(1, c, (2,))
         quantize_v(7)

@@ -23,10 +23,10 @@ QUARTER = HALF // 2
 H_VECTOR = 320
 
 G_BANKS = ("bank0", "bank1", "bank2", "bank3")
-V_BANKS = ("bank4", "bank5")
-T_BANKS = ("bank6", "bank7")
+X_BANKS = ("bank4", "bank5", "bank6", "bank7")
 
 UNITS = ((0, 0), (1, 0), (0, 1), (1, 1), (2, 0), (3, 0), (2, 1), (3, 1))
+LAST = len(UNITS) - 1
 
 
 def tile_mpc_box_step_s7_kernel(tc, u, h, lo, hi, psi_bytes, psi_scale, out):
@@ -37,10 +37,8 @@ def tile_mpc_box_step_s7_kernel(tc, u, h, lo, hi, psi_bytes, psi_scale, out):
         psum = ctx.enter_context(tc.psum_pool(name="psum", bufs=1))
         ctx.enter_context(tc.manual_schedule())
 
-        ident_f32 = keep.tile([P, P], F32, name="ident_f32")
-        make_identity(nc, ident_f32[:])
-        ident_bf = keep.tile([P, P], BF16, name="ident_bf")
-        make_identity(nc, ident_bf[:])
+        ident = keep.tile([P, P], F32, name="ident")
+        make_identity(nc, ident[:])
 
         u_sb, lo_sb, hi_sb, h_raw, bytes_sb = {}, {}, {}, {}, {}
         h_codes, h_scales, u_codes, u_scales = {}, {}, {}, {}
@@ -80,22 +78,11 @@ def tile_mpc_box_step_s7_kernel(tc, u, h, lo, hi, psi_bytes, psi_scale, out):
                 out=pool_codes[key][:].bitcast(FP8X4), scales=pool_scales[key][:], in_=grouped
             )
 
-        def interleave(engine_copy, dst, src, c0, c1):
-            engine_copy(out=dst[:, c0:c1, :], in_=src[:, :, c0:c1].rearrange("p t n -> p n t"))
-
-        def interleave_pe(bank, src, first):
-            half = P
-            ps = psum.tile([P, QUARTER, PACK], BF16, name="il_" + bank, tag=bank)
-            for s in range(QUARTER // half):
-                c0 = first + s * half
-                nc.tensor.matmul(
-                    out=ps[:, s * half : (s + 1) * half, :],
-                    lhsT=ident_bf[:],
-                    rhs=src[:, :, c0 : c0 + half].rearrange("p t n -> p n t"),
-                    start=True,
-                    stop=True,
-                )
-            return ps
+        def interleave(engine_copy, dst, src):
+            engine_copy(
+                out=dst.rearrange("p (c i) t -> p c t i", i=4),
+                in_=src.rearrange("p t (c i) -> p c t i", i=4),
+            )
 
         def grouped_tile(name):
             return work.tile([P, HALF, PACK], BF16, name=name, tag="grouped", bufs=3, align_bytes=64)
@@ -103,28 +90,35 @@ def tile_mpc_box_step_s7_kernel(tc, u, h, lo, hi, psi_bytes, psi_scale, out):
         def flat(t):
             return t[:].rearrange("p n t -> p (n t)")
 
-        xt = {}
         ut = {}
 
-        def transpose_u(j, bank):
+        def turn_u(j, bank):
             g, t = divmod(j, PACK)
             words = u_sb[g][:, t, :].bitcast(F32)
-            xt[j] = psum.tile([P, 2, 2, P], F32, name="xt%d" % j, tag=bank)
+            xt = psum.tile([P, 2, 2, P], F32, name="xt%d" % j, tag=bank)
             for k in range(2):
                 for w in range(2):
                     nc.tensor.transpose(
-                        xt[j][:, k, w, :],
-                        words[:, 256 * k + w : 256 * (k + 1) : 2],
-                        ident_f32[:],
+                        xt[:, k, w, :], words[:, 256 * k + w : 256 * (k + 1) : 2], ident[:]
                     )
+            if j % 2 == 0:
+                ut[j // 2] = work.tile([P, 2, 2, P, 2], F32, name="ut%d" % j, tag="ut", bufs=3, align_bytes=64)
+            nc.scalar.copy(out=ut[j // 2][:, j % 2], in_=xt[:].rearrange("p k w r -> p k r w"))
 
-        def copy_ut(j):
-            ut[j] = work.tile([P, 2, P, 2], F32, name="ut%d" % j, tag="ut", bufs=4, align_bytes=64)
-            nc.scalar.copy(out=ut[j][:], in_=xt[j][:].rearrange("p k w r -> p k r w"))
+        def quantize_u_one(j):
+            if j % 2 == 0:
+                u_codes[j // 2] = keep.tile([P, 4 * P], U32, name="c_u%d" % j, align_bytes=64)
+                u_scales[j // 2] = keep.tile([P, 4 * P], U8, name="s_u%d" % j, align_bytes=64)
+            w = slice(j % 2 * 2 * P, (j % 2 + 1) * 2 * P)
+            nc.vector.quantize_mx(
+                out=u_codes[j // 2][:, w].bitcast(FP8X4),
+                scales=u_scales[j // 2][:, w],
+                in_=ut[j // 2][:, j % 2].rearrange("p k r w -> p (k r w)").bitcast(BF16),
+            )
 
-        def quantize_u(j):
-            grouped = ut[j][:].rearrange("p k r w -> p (k r w)").bitcast(BF16)
-            quantize("u%d" % j, u_codes, u_scales, j, grouped, 2 * P)
+        def quantize_u_pair(j2):
+            grouped = ut[j2][:].rearrange("p s k r w -> p (s k r w)").bitcast(BF16)
+            quantize("u%d" % (2 * j2), u_codes, u_scales, j2, grouped, 4 * P)
 
         g_ps = {}
 
@@ -133,64 +127,55 @@ def tile_mpc_box_step_s7_kernel(tc, u, h, lo, hi, psi_bytes, psi_scale, out):
             j = g * PACK + t
             g_ps[i, t] = psum.tile([P, HALF], F32, name="g%d%d" % (i, t), tag=G_BANKS[t])
             for k in range(2):
+                w = slice((j % 2 * 2 + k) * P, (j % 2 * 2 + k + 1) * P)
                 nc.tensor.matmul_mx(
                     out=g_ps[i, t][:],
-                    lhsT=u_codes[j][:, k * P : (k + 1) * P].bitcast(FP8X4),
-                    lhsT_scale=u_scales[j][:, k * P : (k + 1) * P],
+                    lhsT=u_codes[j // 2][:, w].bitcast(FP8X4),
+                    lhsT_scale=u_scales[j // 2][:, w],
                     rhs=h_codes[k, n][:].bitcast(FP8X4),
                     rhs_scale=h_scales[k, n][:],
                     start=(k == 0),
                     stop=(k == 1),
                 )
 
-        d_sb, m_sb, v_sb, vp, vg = {}, {}, {}, {}, {}
+        d_sb, m_sb, v_sb, vg = {}, {}, {}, {}
 
         def sub(i, t):
             g, n = UNITS[i]
             if t == 0:
-                d_sb[i] = work.tile([P, 2, PACK, QUARTER], BF16, name="d%d" % i, tag="d", bufs=2)
+                d_sb[i] = work.tile([P, PACK, HALF], BF16, name="d%d" % i, tag="d", bufs=2)
             nc.vector.tensor_tensor(
-                out=d_sb[i][:, :, t, :],
-                in0=u_sb[g][:, t, n * HALF : (n + 1) * HALF].rearrange("p (q n) -> p q n", q=2),
-                in1=g_ps[i, t][:].rearrange("p (q n) -> p q n", q=2),
+                out=d_sb[i][:, t, :],
+                in0=u_sb[g][:, t, n * HALF : (n + 1) * HALF],
+                in1=g_ps[i, t][:],
                 op=ALU.subtract,
             )
 
-        def clamp_lo(i, q):
-            if q == 0:
-                m_sb[i] = work.tile([P, 2, PACK, QUARTER], BF16, name="m%d" % i, tag="m", bufs=2)
-            cols = slice(q * QUARTER, (q + 1) * QUARTER)
-            nc.vector.tensor_tensor(
-                out=m_sb[i][:, q, :, :], in0=d_sb[i][:, q, :, :], in1=lo_sb[UNITS[i]][:, :, cols], op=ALU.max
-            )
+        def clamp_lo(i):
+            m_sb[i] = work.tile([P, PACK, HALF], BF16, name="m%d" % i, tag="m", bufs=2)
+            nc.vector.tensor_tensor(out=m_sb[i][:], in0=d_sb[i][:], in1=lo_sb[UNITS[i]][:], op=ALU.max)
 
         def clamp_hi(i, q):
             v_sb[i, q] = work.tile([P, PACK, QUARTER], BF16, name="v%d%d" % (i, q), tag="v", bufs=4)
             cols = slice(q * QUARTER, (q + 1) * QUARTER)
             nc.vector.tensor_tensor(
-                out=v_sb[i, q][:], in0=m_sb[i][:, q, :, :], in1=hi_sb[UNITS[i]][:, :, cols], op=ALU.min
+                out=v_sb[i, q][:], in0=m_sb[i][:, :, cols], in1=hi_sb[UNITS[i]][:, :, cols], op=ALU.min
             )
 
-        def v_tile(i, q):
+        def group_v(i, q, engine_copy):
             if q == 0:
                 vg[i] = work.tile([P, HALF, PACK], BF16, name="vg%d" % i, tag="vg", bufs=2, align_bytes=64)
-            return vg[i][:, q * QUARTER : (q + 1) * QUARTER, :]
-
-        def v_interleave(i, q):
-            vp[i, q] = interleave_pe(V_BANKS[q], v_sb[i, q], 0)
-            nc.scalar.copy(out=v_tile(i, q), in_=vp[i, q][:])
-
-        def v_direct(i, q, engine_copy):
-            engine_copy(out=v_tile(i, q), in_=v_sb[i, q][:].rearrange("p t n -> p n t"))
+            interleave(engine_copy, vg[i][:, q * QUARTER : (q + 1) * QUARTER, :], v_sb[i, q][:])
 
         def quantize_v(i):
             quantize("v%d" % i, v_codes, v_scales, UNITS[i], flat(vg[i]), HALF)
 
         planes, pg = {}, {}
 
-        def psi_widen(g):
-            planes[g] = work.tile([P, PACK, C], BF16, name="planes%d" % g, tag="planes", bufs=2)
-            for t in range(PACK):
+        def widen_psi(g, first=0, last=PACK):
+            if first == 0:
+                planes[g] = work.tile([P, PACK, C], BF16, name="planes%d" % g, tag="planes", bufs=2)
+            for t in range(first, last):
                 nc.scalar.activation(
                     out=planes[g][:, t, :],
                     in_=bytes_sb[g][:, t * C : (t + 1) * C].bitcast(FP8),
@@ -198,26 +183,21 @@ def tile_mpc_box_step_s7_kernel(tc, u, h, lo, hi, psi_bytes, psi_scale, out):
                     scale=scale_sb[:, g, t : t + 1],
                 )
 
-        def psi_interleave(g):
+        def group_psi(g, engine_copy, parts):
             pg[g] = grouped_tile("pg%d" % g)
-            interleave(nc.scalar.copy, pg[g], planes[g], 0, QUARTER)
-            interleave(nc.scalar.copy, pg[g], planes[g], QUARTER, HALF)
-
-        def psi_interleave_pe(g):
-            pg[g] = grouped_tile("pg%d" % g)
-            for q in range(2):
-                ps = interleave_pe(V_BANKS[q], planes[g], q * QUARTER)
-                nc.scalar.copy(out=pg[g][:, q * QUARTER : (q + 1) * QUARTER, :], in_=ps[:])
+            w = HALF // parts
+            for s in range(parts):
+                cols = slice(s * w, (s + 1) * w)
+                interleave(engine_copy, pg[g][:, cols, :], planes[g][:, :, cols])
 
         def quantize_psi(g):
             quantize("psi%d" % g, psi_codes, psi_scales, g, flat(pg[g]), C)
 
         acc = {}
 
-        def stage2_open(n, c, bank):
-            acc[n, c] = psum.tile([P, HALF], F32, name="acc%d%d" % (n, c), tag=bank)
-
-        def stage2(n, c, groups):
+        def stage2(n, c, bank, groups):
+            if groups[0] == 0:
+                acc[n, c] = psum.tile([P, HALF], F32, name="acc%d%d" % (n, c), tag=bank)
             for g in groups:
                 nc.tensor.matmul_mx(
                     out=acc[n, c][:],
@@ -247,15 +227,16 @@ def tile_mpc_box_step_s7_kernel(tc, u, h, lo, hi, psi_bytes, psi_scale, out):
         load_psi(0)
         load_box(0, 0)
         alloc_u(1)
-        for t in range(PACK):
-            load_u(1, t, t + 1)
+        load_u(1, 0, 2)
+        load_u(1, 2, 4)
         load_h(0, 1)
         load_h(1, 1)
         load_box(1, 0)
-        load_box(0, 1)
-        load_psi(1)
         alloc_u(2)
-        load_u(2, 0, PACK)
+        load_u(2, 0, 2)
+        load_box(0, 1)
+        load_u(2, 2, 4)
+        load_psi(1)
         load_box(1, 1)
         load_psi(2)
         load_box(2, 0)
@@ -264,164 +245,123 @@ def tile_mpc_box_step_s7_kernel(tc, u, h, lo, hi, psi_bytes, psi_scale, out):
         hg = {}
         hg[0] = grouped_tile("hg00")
         hg[1] = grouped_tile("hg10")
-        transpose_u(0, T_BANKS[0])
-        copy_ut(0)
-        interleave(nc.vector.tensor_copy, hg[0], h_raw[0, 0], 0, H_VECTOR)
-        interleave(nc.scalar.copy, hg[0], h_raw[0, 0], H_VECTOR, HALF)
-        quantize_u(0)
-        interleave(nc.vector.tensor_copy, hg[1], h_raw[1, 0], 0, H_VECTOR)
-        interleave(nc.scalar.copy, hg[1], h_raw[1, 0], H_VECTOR, HALF)
-        transpose_u(1, T_BANKS[1])
-        copy_ut(1)
-        quantize("h00", h_codes, h_scales, (0, 0), flat(hg[0]), HALF)
-        transpose_u(2, V_BANKS[0])
-        copy_ut(2)
-        quantize("h10", h_codes, h_scales, (1, 0), flat(hg[1]), HALF)
-        transpose_u(3, V_BANKS[1])
-        copy_ut(3)
-        stage1(0, 0)
-        quantize_u(1)
-        stage1(0, 1)
-        quantize_u(2)
-        stage1(0, 2)
-        psi_widen(0)
 
+        def group_h_shared(k):
+            interleave(nc.vector.tensor_copy, hg[k][:, :H_VECTOR, :], h_raw[k, 0][:, :, :H_VECTOR])
+            interleave(nc.scalar.copy, hg[k][:, H_VECTOR:, :], h_raw[k, 0][:, :, H_VECTOR:])
+
+        turn_u(0, X_BANKS[0])
+        group_h_shared(0)
+        quantize_u_one(0)
+        group_h_shared(1)
+        turn_u(1, X_BANKS[1])
+        quantize("h00", h_codes, h_scales, (0, 0), flat(hg[0]), HALF)
+        turn_u(2, X_BANKS[2])
+        quantize("h10", h_codes, h_scales, (1, 0), flat(hg[1]), HALF)
+        turn_u(3, X_BANKS[3])
+        stage1(0, 0)
+        quantize_u_one(1)
+        stage1(0, 1)
+        quantize_u_one(2)
+        stage1(0, 2)
+        widen_psi(0)
         sub(0, 0)
-        quantize_u(3)
+        quantize_u_one(3)
         stage1(0, 3)
+        for j in (4, 5, 6, 7):
+            turn_u(j, X_BANKS[j % 4])
         sub(0, 1)
         sub(0, 2)
-        for s, j in enumerate((4, 5, 6, 7)):
-            transpose_u(j, T_BANKS[s % 2])
-            copy_ut(j)
         sub(0, 3)
-        clamp_lo(0, 0)
-        clamp_lo(0, 1)
-        quantize_u(4)
-        stage1(1, 0)
-        clamp_hi(0, 0)
-        v_interleave(0, 0)
-        quantize_u(5)
-        stage1(1, 1)
-        clamp_hi(0, 1)
-        v_interleave(0, 1)
-        quantize_u(6)
-        stage1(1, 2)
-        quantize_u(7)
-        stage1(1, 3)
-        hg[2] = grouped_tile("hg01")
-        interleave(nc.scalar.copy, hg[2], h_raw[0, 1], 0, QUARTER)
-        interleave(nc.scalar.copy, hg[2], h_raw[0, 1], QUARTER, HALF)
         hg[3] = grouped_tile("hg11")
+        clamp_lo(0)
+        quantize_u_pair(2)
+        stage1(1, 0)
+        stage1(1, 1)
+        clamp_hi(0, 0)
+        group_v(0, 0, nc.scalar.copy)
+        quantize_u_pair(3)
+        stage1(1, 2)
+        stage1(1, 3)
+        clamp_hi(0, 1)
+        group_v(0, 1, nc.scalar.copy)
+        hg[2] = grouped_tile("hg01")
         for q in range(2):
-            ps = interleave_pe(T_BANKS[q], h_raw[1, 1], q * QUARTER)
-            nc.scalar.copy(out=hg[3][:, q * QUARTER : (q + 1) * QUARTER, :], in_=ps[:])
+            cols = slice(q * QUARTER, (q + 1) * QUARTER)
+            interleave(nc.scalar.copy, hg[2][:, cols, :], h_raw[0, 1][:, :, cols])
+        interleave(nc.vector.tensor_copy, hg[3][:], h_raw[1, 1][:])
 
-        def nothing():
-            return None
+        def accumulate(n, banks, groups):
+            for c in range(4):
+                stage2(n, c, banks[c], groups)
 
-        def body(i, tiles=(), scalar_work=nothing, early_q=nothing, mid_q=nothing, late_q=nothing, pe_work=nothing, pe_mid=nothing, pe_late=nothing):
-            for s, j in enumerate(tiles):
-                transpose_u(j, T_BANKS[s % 2])
-                copy_ut(j)
+        pairs = {1: (4,), 2: (5,), 3: (6, 7)}
+        for i in range(1, LAST + 1):
+            for k, pair in enumerate(pairs.get(i, ())):
+                turn_u(2 * pair, X_BANKS[2 * k])
+                turn_u(2 * pair + 1, X_BANKS[2 * k + 1])
             for t in range(PACK):
                 sub(i, t)
-            early_q()
-            if i not in (1, 7):
+            if i == 1:
+                group_psi(0, nc.scalar.copy, 2)
+            if i == 2:
+                widen_psi(1)
+            if i == 3:
+                widen_psi(2, 0, 2)
+            if i == 4:
+                group_psi(1, nc.scalar.copy, 2)
+                widen_psi(2, 2, 4)
+            if i == 5:
+                group_psi(2, nc.scalar.copy, 2)
+                widen_psi(3, 0, 2)
+            if i == 6:
+                widen_psi(3, 2, 4)
+            if i not in (1, LAST):
                 for t in range(PACK):
                     stage1(i + 1, t)
-            pe_work()
-            scalar_work()
-            clamp_lo(i, 0)
-            clamp_lo(i, 1)
-            if i == 1:
-                quantize("h01", h_codes, h_scales, (0, 1), flat(hg[2]), HALF)
-            quantize_v(i - 1)
+            if i == 5:
+                accumulate(0, X_BANKS, (0, 1))
+            if i == 6:
+                accumulate(0, X_BANKS, (2,))
+            if i == LAST:
+                accumulate(1, G_BANKS, (0, 1))
+                quantize_psi(3)
+                accumulate(0, X_BANKS, (3,))
+                for c in range(4):
+                    store(0, c, nc.scalar.copy)
+            clamp_lo(i)
             if i == 1:
                 quantize("h11", h_codes, h_scales, (1, 1), flat(hg[3]), HALF)
+            if i == 6:
+                group_psi(3, nc.vector.tensor_copy, 1)
+            if i == LAST:
+                clamp_hi(i, 0)
+                group_v(i, 0, nc.scalar.copy)
+            quantize_v(i - 1)
+            if i == 1:
+                quantize("h01", h_codes, h_scales, (0, 1), flat(hg[2]), HALF)
                 for t in range(PACK):
                     stage1(i + 1, t)
-            pe_mid()
-            clamp_hi(i, 0)
-            if i < 6:
-                v_interleave(i, 0)
-            else:
-                v_direct(i, 0, nc.scalar.copy)
-            mid_q()
+            if i < LAST:
+                clamp_hi(i, 0)
+                group_v(i, 0, nc.scalar.copy)
             clamp_hi(i, 1)
-            if i < 6:
-                v_interleave(i, 1)
-            else:
-                v_direct(i, 1, nc.scalar.copy)
-            pe_late()
-            late_q()
+            group_v(i, 1, nc.scalar.copy if i < LAST else nc.vector.tensor_copy)
+            for pair in pairs.get(i, ()):
+                quantize_u_pair(pair)
+            if i in (2, 4, 5):
+                quantize_psi({2: 0, 4: 1, 5: 2}[i])
+            if i == 2:
+                alloc_u(3)
+                load_u(3, 0, 2)
+                load_u(3, 2, 4)
+                load_box(3, 0)
+            if i == 3:
+                load_box(2, 1)
+                load_box(3, 1)
 
-        body(1, scalar_work=lambda: psi_interleave(0))
-        body(
-            2,
-            tiles=(8, 9, 10, 11),
-            scalar_work=lambda: psi_widen(1),
-            early_q=lambda: quantize_psi(0),
-            mid_q=lambda: quantize_u(8),
-            late_q=lambda: [quantize_u(j) for j in (9, 10, 11)],
-        )
-        alloc_u(3)
-        load_u(3, 0, PACK)
-        load_box(3, 0)
-        body(
-            3,
-            tiles=(12, 13, 14, 15),
-            scalar_work=lambda: psi_interleave(1),
-            early_q=lambda: quantize_u(12),
-            mid_q=lambda: quantize_u(13),
-            late_q=lambda: [quantize_u(j) for j in (14, 15)],
-        )
-        load_box(2, 1)
-        load_box(3, 1)
-
-        def psi_work(g):
-            psi_widen(g)
-            psi_interleave_pe(g)
-
-        body(4, early_q=lambda: quantize_psi(1), scalar_work=lambda: psi_work(2))
-
-        def half0_first():
-            for c in range(2):
-                stage2_open(0, c, T_BANKS[c])
-                stage2(0, c, (0, 1))
-
-        body(5, early_q=lambda: quantize_psi(2), scalar_work=lambda: psi_work(3), pe_work=half0_first)
-
-        def half0_close():
-            for c in range(2):
-                stage2(0, c, (2, 3))
-                store(0, c, nc.scalar.copy)
-
-        def half0_second():
-            for c in range(2, 4):
-                stage2_open(0, c, T_BANKS[c - 2])
-                stage2(0, c, (0, 1))
-
-        body(6, early_q=lambda: quantize_psi(3), pe_mid=half0_close, pe_late=half0_second)
-
-        for t in range(PACK):
-            sub(7, t)
-        for c in range(2, 4):
-            stage2(0, c, (2, 3))
-            store(0, c, nc.scalar.copy)
+        accumulate(1, G_BANKS, (2,))
+        quantize_v(LAST)
         for c in range(4):
-            stage2_open(1, c, G_BANKS[c])
-            stage2(1, c, (0, 1))
-        clamp_lo(7, 0)
-        clamp_lo(7, 1)
-        quantize_v(6)
-        clamp_hi(7, 0)
-        v_direct(7, 0, nc.scalar.copy)
-        clamp_hi(7, 1)
-        v_direct(7, 1, nc.vector.tensor_copy)
-        for c in range(4):
-            stage2(1, c, (2,))
-        quantize_v(7)
-        for c in range(4):
-            stage2(1, c, (3,))
+            stage2(1, c, G_BANKS[c], (3,))
             store(1, c, nc.scalar.copy if c % 2 == 0 else nc.vector.tensor_copy)

@@ -39,6 +39,8 @@ def tile_mpc_box_step_s7_kernel(tc, u, h, lo, hi, psi_bytes, psi_scale, out):
 
         ident = keep.tile([P, P], F32, name="ident")
         make_identity(nc, ident[:])
+        ident_bf = keep.tile([P, P], BF16, name="ident_bf")
+        make_identity(nc, ident_bf[:])
 
         u_sb, lo_sb, hi_sb, h_raw, bytes_sb = {}, {}, {}, {}, {}
         h_codes, h_scales, u_codes, u_scales = {}, {}, {}, {}
@@ -48,20 +50,20 @@ def tile_mpc_box_step_s7_kernel(tc, u, h, lo, hi, psi_bytes, psi_scale, out):
             return x[g * GROUP : (g + 1) * GROUP, :].rearrange("(p t) n -> p t n", t=PACK)
 
         def alloc_u(g):
-            u_sb[g] = work.tile([P, PACK, K], BF16, name="u%d" % g, tag="u", bufs=3)
+            u_sb[g] = work.tile([P, PACK, K], BF16, name="u%d" % g, tag="u", bufs=4)
 
         def load_u(g, t0, t1):
             nc.sync.dma_start(out=u_sb[g][:, t0:t1, :], in_=rows(u, g)[:, t0:t1, :])
 
         def load_box(g, n):
             cols = slice(n * HALF, (n + 1) * HALF)
-            lo_sb[g, n] = work.tile([P, PACK, HALF], BF16, name="lo%d%d" % (g, n), tag="lo", bufs=6)
+            lo_sb[g, n] = work.tile([P, PACK, HALF], BF16, name="lo%d%d" % (g, n), tag="rows", bufs=16)
             nc.sync.dma_start(out=lo_sb[g, n][:], in_=rows(lo, g)[:, :, cols])
-            hi_sb[g, n] = work.tile([P, PACK, HALF], BF16, name="hi%d%d" % (g, n), tag="hi", bufs=6)
+            hi_sb[g, n] = work.tile([P, PACK, HALF], BF16, name="hi%d%d" % (g, n), tag="rows", bufs=16)
             nc.sync.dma_start(out=hi_sb[g, n][:], in_=rows(hi, g)[:, :, cols])
 
         def load_h(k, n):
-            h_raw[k, n] = work.tile([P, PACK, HALF], BF16, name="h%d%d" % (k, n), tag="h_raw", bufs=4)
+            h_raw[k, n] = work.tile([P, PACK, HALF], BF16, name="h%d%d" % (k, n), tag="rows", bufs=16)
             nc.sync.dma_start(out=h_raw[k, n][:], in_=rows(h, k)[:, :, n * HALF : (n + 1) * HALF])
 
         def load_psi(g):
@@ -138,7 +140,7 @@ def tile_mpc_box_step_s7_kernel(tc, u, h, lo, hi, psi_bytes, psi_scale, out):
                     stop=(k == 1),
                 )
 
-        d_sb, m_sb, v_sb, vg = {}, {}, {}, {}
+        d_sb, v_sb, vg = {}, {}, {}
 
         def sub(i, t):
             g, n = UNITS[i]
@@ -151,15 +153,15 @@ def tile_mpc_box_step_s7_kernel(tc, u, h, lo, hi, psi_bytes, psi_scale, out):
                 op=ALU.subtract,
             )
 
-        def clamp_lo(i):
-            m_sb[i] = work.tile([P, PACK, HALF], BF16, name="m%d" % i, tag="m", bufs=2)
-            nc.vector.tensor_tensor(out=m_sb[i][:], in0=d_sb[i][:], in1=lo_sb[UNITS[i]][:], op=ALU.max)
+        def clamp_lo(i, cols=slice(0, HALF)):
+            part = d_sb[i][:, :, cols]
+            nc.vector.tensor_tensor(out=part, in0=part, in1=lo_sb[UNITS[i]][:, :, cols], op=ALU.max)
 
         def clamp_hi(i, q):
             v_sb[i, q] = work.tile([P, PACK, QUARTER], BF16, name="v%d%d" % (i, q), tag="v", bufs=4)
             cols = slice(q * QUARTER, (q + 1) * QUARTER)
             nc.vector.tensor_tensor(
-                out=v_sb[i, q][:], in0=m_sb[i][:, :, cols], in1=hi_sb[UNITS[i]][:, :, cols], op=ALU.min
+                out=v_sb[i, q][:], in0=d_sb[i][:, :, cols], in1=hi_sb[UNITS[i]][:, :, cols], op=ALU.min
             )
 
         def group_v(i, q, engine_copy):
@@ -170,7 +172,19 @@ def tile_mpc_box_step_s7_kernel(tc, u, h, lo, hi, psi_bytes, psi_scale, out):
         def quantize_v(i):
             quantize("v%d" % i, v_codes, v_scales, UNITS[i], flat(vg[i]), HALF)
 
-        planes, pg = {}, {}
+        def quantize_v_half(i, q):
+            key = UNITS[i]
+            if q == 0:
+                v_codes[key] = keep.tile([P, HALF], U32, name="c_v%d" % i, align_bytes=64)
+                v_scales[key] = keep.tile([P, HALF], U8, name="s_v%d" % i, align_bytes=64)
+            cols = slice(q * QUARTER, (q + 1) * QUARTER)
+            nc.vector.quantize_mx(
+                out=v_codes[key][:, cols].bitcast(FP8X4),
+                scales=v_scales[key][:, cols],
+                in_=vg[i][:, cols, :].rearrange("p n t -> p (n t)"),
+            )
+
+        planes, pg, pp = {}, {}, {}
 
         def widen_psi(g, first=0, last=PACK):
             if first == 0:
@@ -183,36 +197,59 @@ def tile_mpc_box_step_s7_kernel(tc, u, h, lo, hi, psi_bytes, psi_scale, out):
                     scale=scale_sb[:, g, t : t + 1],
                 )
 
-        def group_psi(g, engine_copy, parts):
+        def group_psi_scalar(g):
             pg[g] = grouped_tile("pg%d" % g)
-            w = HALF // parts
-            for s in range(parts):
-                cols = slice(s * w, (s + 1) * w)
-                interleave(engine_copy, pg[g][:, cols, :], planes[g][:, :, cols])
+            for q in range(2):
+                cols = slice(q * QUARTER, (q + 1) * QUARTER)
+                interleave(nc.scalar.copy, pg[g][:, cols, :], planes[g][:, :, cols])
+
+        def group_psi(g):
+            for q in range(2):
+                ps = psum.tile([P, QUARTER, PACK], BF16, name="pp%d%d" % (g, q), tag=X_BANKS[q])
+                pp[g, q] = ps
+                for s in range(2):
+                    first = q * QUARTER + s * P
+                    nc.tensor.matmul(
+                        out=ps[:, s * P : (s + 1) * P, :],
+                        lhsT=ident_bf[:],
+                        rhs=planes[g][:, :, first : first + P].rearrange("p t c -> p c t"),
+                        start=True,
+                        stop=True,
+                    )
+
+        def copy_psi(g):
+            pg[g] = grouped_tile("pg%d" % g)
+            for q in range(2):
+                nc.scalar.copy(out=pg[g][:, q * QUARTER : (q + 1) * QUARTER, :], in_=pp[g, q][:])
 
         def quantize_psi(g):
             quantize("psi%d" % g, psi_codes, psi_scales, g, flat(pg[g]), C)
 
         acc = {}
 
-        def stage2(n, c, bank, groups):
+        def stage2(n, c, cols, bank, groups):
+            key = n, c, cols.start
+            width = cols.stop - cols.start
             if groups[0] == 0:
-                acc[n, c] = psum.tile([P, HALF], F32, name="acc%d%d" % (n, c), tag=bank)
+                acc[key] = psum.tile([P, width], F32, name="acc%d%d%d" % key, tag=bank)
             for g in groups:
                 nc.tensor.matmul_mx(
-                    out=acc[n, c][:],
+                    out=acc[key][:],
                     lhsT=psi_codes[g][:, c * P : (c + 1) * P].bitcast(FP8X4),
                     lhsT_scale=psi_scales[g][:, c * P : (c + 1) * P],
-                    rhs=v_codes[g, n][:].bitcast(FP8X4),
-                    rhs_scale=v_scales[g, n][:],
+                    rhs=v_codes[g, n][:, cols].bitcast(FP8X4),
+                    rhs_scale=v_scales[g, n][:, cols],
                     start=(g == 0),
                     stop=(g == 3),
                 )
 
-        def store(n, c, engine_copy):
-            res = work.tile([P, HALF], F32, name="res%d%d" % (n, c), tag="res", bufs=4)
-            engine_copy(out=res[:], in_=acc[n, c][:])
-            nc.sync.dma_start(out=out[c * P : (c + 1) * P, n * HALF : (n + 1) * HALF], in_=res[:])
+        def store(n, c, cols, engine_copy, tag, bufs):
+            key = n, c, cols.start
+            width = cols.stop - cols.start
+            res = work.tile([P, width], F32, name="res%d%d%d" % key, tag=tag, bufs=bufs)
+            engine_copy(out=res[:], in_=acc[key][:])
+            first = n * HALF + cols.start
+            nc.sync.dma_start(out=out[c * P : (c + 1) * P, first : first + width], in_=res[:])
 
         alloc_u(0)
         load_u(0, 0, 1)
@@ -238,8 +275,11 @@ def tile_mpc_box_step_s7_kernel(tc, u, h, lo, hi, psi_bytes, psi_scale, out):
         load_u(2, 2, 4)
         load_psi(1)
         load_box(1, 1)
-        load_psi(2)
+        alloc_u(3)
+        load_u(3, 0, PACK)
         load_box(2, 0)
+        load_psi(2)
+        load_box(3, 0)
         load_psi(3)
 
         hg = {}
@@ -291,77 +331,88 @@ def tile_mpc_box_step_s7_kernel(tc, u, h, lo, hi, psi_bytes, psi_scale, out):
             interleave(nc.scalar.copy, hg[2][:, cols, :], h_raw[0, 1][:, :, cols])
         interleave(nc.vector.tensor_copy, hg[3][:], h_raw[1, 1][:])
 
-        def accumulate(n, banks, groups):
+        whole, quarter = slice(0, HALF), (slice(0, QUARTER), slice(QUARTER, HALF))
+
+        def accumulate(n, cols, banks, groups):
             for c in range(4):
-                stage2(n, c, banks[c], groups)
+                stage2(n, c, cols, banks[c], groups)
 
         pairs = {1: (4,), 2: (5,), 3: (6, 7)}
-        for i in range(1, LAST + 1):
+        for i in range(1, LAST):
             for k, pair in enumerate(pairs.get(i, ())):
                 turn_u(2 * pair, X_BANKS[2 * k])
                 turn_u(2 * pair + 1, X_BANKS[2 * k + 1])
             for t in range(PACK):
                 sub(i, t)
             if i == 1:
-                group_psi(0, nc.scalar.copy, 2)
+                group_psi_scalar(0)
             if i == 2:
                 widen_psi(1)
             if i == 3:
                 widen_psi(2, 0, 2)
             if i == 4:
-                group_psi(1, nc.scalar.copy, 2)
                 widen_psi(2, 2, 4)
             if i == 5:
-                group_psi(2, nc.scalar.copy, 2)
-                widen_psi(3, 0, 2)
+                widen_psi(3)
             if i == 6:
-                widen_psi(3, 2, 4)
-            if i not in (1, LAST):
+                group_psi_scalar(3)
+            if i != 1:
                 for t in range(PACK):
                     stage1(i + 1, t)
-            if i == 5:
-                accumulate(0, X_BANKS, (0, 1))
+            if i in (4, 5):
+                group_psi({4: 1, 5: 2}[i])
             if i == 6:
-                accumulate(0, X_BANKS, (2,))
-            if i == LAST:
-                accumulate(1, G_BANKS, (0, 1))
-                quantize_psi(3)
-                accumulate(0, X_BANKS, (3,))
-                for c in range(4):
-                    store(0, c, nc.scalar.copy)
-            clamp_lo(i)
+                accumulate(0, whole, X_BANKS, (0, 1))
             if i == 1:
                 quantize("h11", h_codes, h_scales, (1, 1), flat(hg[3]), HALF)
-            if i == 6:
-                group_psi(3, nc.vector.tensor_copy, 1)
-            if i == LAST:
-                clamp_hi(i, 0)
-                group_v(i, 0, nc.scalar.copy)
-            quantize_v(i - 1)
+            else:
+                quantize_v(i - 1)
+            clamp_lo(i)
             if i == 1:
+                quantize_v(0)
                 quantize("h01", h_codes, h_scales, (0, 1), flat(hg[2]), HALF)
                 for t in range(PACK):
                     stage1(i + 1, t)
-            if i < LAST:
-                clamp_hi(i, 0)
-                group_v(i, 0, nc.scalar.copy)
-            clamp_hi(i, 1)
-            group_v(i, 1, nc.scalar.copy if i < LAST else nc.vector.tensor_copy)
             for pair in pairs.get(i, ()):
                 quantize_u_pair(pair)
-            if i in (2, 4, 5):
-                quantize_psi({2: 0, 4: 1, 5: 2}[i])
-            if i == 2:
-                alloc_u(3)
-                load_u(3, 0, 2)
-                load_u(3, 2, 4)
-                load_box(3, 0)
-            if i == 3:
+            if i in (2, 5, 6):
+                quantize_psi({2: 0, 5: 1, 6: 2}[i])
+            if i == 6:
+                accumulate(0, whole, X_BANKS, (2,))
+            clamp_hi(i, 0)
+            group_v(i, 0, nc.scalar.copy)
+            clamp_hi(i, 1)
+            group_v(i, 1, nc.scalar.copy)
+            if i in (4, 5):
+                copy_psi({4: 1, 5: 2}[i])
+            if i == 1:
                 load_box(2, 1)
                 load_box(3, 1)
 
-        accumulate(1, G_BANKS, (2,))
-        quantize_v(LAST)
+        for t in range(PACK):
+            sub(LAST, t)
+        quantize_psi(3)
+        accumulate(0, whole, X_BANKS, (3,))
         for c in range(4):
-            stage2(1, c, G_BANKS[c], (3,))
-            store(1, c, nc.scalar.copy if c % 2 == 0 else nc.vector.tensor_copy)
+            store(0, c, whole, nc.scalar.copy, "res", 4)
+        for q in range(2):
+            accumulate(1, quarter[q], (G_BANKS, X_BANKS)[q], (0, 1))
+        clamp_lo(LAST, quarter[0])
+        clamp_lo(LAST, quarter[1])
+        quantize_v(LAST - 1)
+        for q in range(2):
+            accumulate(1, quarter[q], (G_BANKS, X_BANKS)[q], (2,))
+        clamp_hi(LAST, 0)
+        clamp_hi(LAST, 1)
+        vg[LAST] = work.tile([P, HALF, PACK], BF16, name="vg_last", tag="vg", bufs=2, align_bytes=64)
+        for q in range(2):
+            for s, engine_copy in enumerate((nc.scalar.copy, nc.vector.tensor_copy)):
+                part = slice(q * QUARTER + s * P, q * QUARTER + (s + 1) * P)
+                interleave(engine_copy, vg[LAST][:, part, :], v_sb[LAST, q][:, :, s * P : (s + 1) * P])
+            quantize_v_half(LAST, q)
+            for c in range(4):
+                stage2(1, c, quarter[q], (G_BANKS, X_BANKS)[q][c], (3,))
+        for c in range(4):
+            store(1, c, quarter[0], nc.scalar.copy, "rows", 16)
+        for c in range(4):
+            store(1, c, quarter[1], nc.vector.tensor_copy if c < 3 else nc.scalar.copy, "rows", 16)

from contextlib import ExitStack

import concourse.mybir as mybir
from concourse.masks import make_identity

B, K, C = 2048, 1024, 512
FLOPS = 2 * B * K * K + 2 * B * K * C

F32 = mybir.dt.float32
BF16 = mybir.dt.bfloat16
U32 = mybir.dt.uint32
U8 = mybir.dt.uint8
FP8 = mybir.dt.float8_e4m3fn
FP8X4 = mybir.dt.float8_e4m3fn_x4
ALU = mybir.AluOpType
COPY = mybir.ActivationFunctionType.Copy

P = 128
PACK = 4
GROUP = P * PACK
HALF = 512
QUARTER = HALF // 2
H_VECTOR = 320

G_BANKS = ("bank0", "bank1", "bank2", "bank3")
X_BANKS = ("bank4", "bank5", "bank6", "bank7")

UNITS = ((0, 0), (1, 0), (0, 1), (1, 1), (2, 0), (3, 0), (2, 1), (3, 1))
LAST = len(UNITS) - 1


def tile_mpc_box_step_s7_kernel(tc, u, h, lo, hi, psi_bytes, psi_scale, out):
    nc = tc.nc
    with ExitStack() as ctx:
        keep = ctx.enter_context(tc.tile_pool(name="keep", bufs=1))
        work = ctx.enter_context(tc.tile_pool(name="work", bufs=2))
        psum = ctx.enter_context(tc.psum_pool(name="psum", bufs=1))
        ctx.enter_context(tc.manual_schedule())

        ident = keep.tile([P, P], F32, name="ident")
        make_identity(nc, ident[:])
        ident_bf = keep.tile([P, P], BF16, name="ident_bf")
        make_identity(nc, ident_bf[:])

        u_sb, lo_sb, hi_sb, h_raw, bytes_sb = {}, {}, {}, {}, {}
        h_codes, h_scales, u_codes, u_scales = {}, {}, {}, {}
        v_codes, v_scales, psi_codes, psi_scales = {}, {}, {}, {}

        def rows(x, g):
            return x[g * GROUP : (g + 1) * GROUP, :].rearrange("(p t) n -> p t n", t=PACK)

        def alloc_u(g):
            u_sb[g] = work.tile([P, PACK, K], BF16, name="u%d" % g, tag="u", bufs=4)

        def load_u(g, t0, t1):
            nc.sync.dma_start(out=u_sb[g][:, t0:t1, :], in_=rows(u, g)[:, t0:t1, :])

        def load_box(g, n):
            cols = slice(n * HALF, (n + 1) * HALF)
            lo_sb[g, n] = work.tile([P, PACK, HALF], BF16, name="lo%d%d" % (g, n), tag="rows", bufs=16)
            nc.sync.dma_start(out=lo_sb[g, n][:], in_=rows(lo, g)[:, :, cols])
            hi_sb[g, n] = work.tile([P, PACK, HALF], BF16, name="hi%d%d" % (g, n), tag="rows", bufs=16)
            nc.sync.dma_start(out=hi_sb[g, n][:], in_=rows(hi, g)[:, :, cols])

        def load_h(k, n):
            h_raw[k, n] = work.tile([P, PACK, HALF], BF16, name="h%d%d" % (k, n), tag="rows", bufs=16)
            nc.sync.dma_start(out=h_raw[k, n][:], in_=rows(h, k)[:, :, n * HALF : (n + 1) * HALF])

        def load_psi(g):
            bytes_sb[g] = keep.tile([P, PACK * C], U8, name="bytes%d" % g)
            nc.sync.dma_start(
                out=bytes_sb[g][:],
                in_=psi_bytes[g * GROUP : (g + 1) * GROUP, :].rearrange("(p t) c -> p (t c)", t=PACK),
            )

        def quantize(name, pool_codes, pool_scales, key, grouped, words):
            pool_codes[key] = keep.tile([P, words], U32, name="c_" + name, align_bytes=64)
            pool_scales[key] = keep.tile([P, words], U8, name="s_" + name, align_bytes=64)
            nc.vector.quantize_mx(
                out=pool_codes[key][:].bitcast(FP8X4), scales=pool_scales[key][:], in_=grouped
            )

        def interleave(engine_copy, dst, src):
            engine_copy(
                out=dst.rearrange("p (c i) t -> p c t i", i=4),
                in_=src.rearrange("p t (c i) -> p c t i", i=4),
            )

        def grouped_tile(name):
            return work.tile([P, HALF, PACK], BF16, name=name, tag="grouped", bufs=3, align_bytes=64)

        def flat(t):
            return t[:].rearrange("p n t -> p (n t)")

        ut = {}

        def turn_u(j, bank):
            g, t = divmod(j, PACK)
            words = u_sb[g][:, t, :].bitcast(F32)
            xt = psum.tile([P, 2, 2, P], F32, name="xt%d" % j, tag=bank)
            for k in range(2):
                for w in range(2):
                    nc.tensor.transpose(
                        xt[:, k, w, :], words[:, 256 * k + w : 256 * (k + 1) : 2], ident[:]
                    )
            if j % 2 == 0:
                ut[j // 2] = work.tile([P, 2, 2, P, 2], F32, name="ut%d" % j, tag="ut", bufs=3, align_bytes=64)
            nc.scalar.copy(out=ut[j // 2][:, j % 2], in_=xt[:].rearrange("p k w r -> p k r w"))

        def quantize_u_one(j):
            if j % 2 == 0:
                u_codes[j // 2] = keep.tile([P, 4 * P], U32, name="c_u%d" % j, align_bytes=64)
                u_scales[j // 2] = keep.tile([P, 4 * P], U8, name="s_u%d" % j, align_bytes=64)
            w = slice(j % 2 * 2 * P, (j % 2 + 1) * 2 * P)
            nc.vector.quantize_mx(
                out=u_codes[j // 2][:, w].bitcast(FP8X4),
                scales=u_scales[j // 2][:, w],
                in_=ut[j // 2][:, j % 2].rearrange("p k r w -> p (k r w)").bitcast(BF16),
            )

        def quantize_u_pair(j2):
            grouped = ut[j2][:].rearrange("p s k r w -> p (s k r w)").bitcast(BF16)
            quantize("u%d" % (2 * j2), u_codes, u_scales, j2, grouped, 4 * P)

        g_ps = {}

        def stage1(i, t):
            g, n = UNITS[i]
            j = g * PACK + t
            g_ps[i, t] = psum.tile([P, HALF], F32, name="g%d%d" % (i, t), tag=G_BANKS[t])
            for k in range(2):
                w = slice((j % 2 * 2 + k) * P, (j % 2 * 2 + k + 1) * P)
                nc.tensor.matmul_mx(
                    out=g_ps[i, t][:],
                    lhsT=u_codes[j // 2][:, w].bitcast(FP8X4),
                    lhsT_scale=u_scales[j // 2][:, w],
                    rhs=h_codes[k, n][:].bitcast(FP8X4),
                    rhs_scale=h_scales[k, n][:],
                    start=(k == 0),
                    stop=(k == 1),
                )

        d_sb, v_sb, vg = {}, {}, {}

        def sub(i, t):
            g, n = UNITS[i]
            if t == 0:
                d_sb[i] = work.tile([P, PACK, HALF], BF16, name="d%d" % i, tag="d", bufs=2)
            nc.vector.tensor_tensor(
                out=d_sb[i][:, t, :],
                in0=u_sb[g][:, t, n * HALF : (n + 1) * HALF],
                in1=g_ps[i, t][:],
                op=ALU.subtract,
            )

        def clamp_lo(i, cols=slice(0, HALF)):
            part = d_sb[i][:, :, cols]
            nc.vector.tensor_tensor(out=part, in0=part, in1=lo_sb[UNITS[i]][:, :, cols], op=ALU.max)

        def clamp_hi(i, q):
            v_sb[i, q] = work.tile([P, PACK, QUARTER], BF16, name="v%d%d" % (i, q), tag="v", bufs=4)
            cols = slice(q * QUARTER, (q + 1) * QUARTER)
            nc.vector.tensor_tensor(
                out=v_sb[i, q][:], in0=d_sb[i][:, :, cols], in1=hi_sb[UNITS[i]][:, :, cols], op=ALU.min
            )

        def group_v(i, q, engine_copy):
            if q == 0:
                vg[i] = work.tile([P, HALF, PACK], BF16, name="vg%d" % i, tag="vg", bufs=2, align_bytes=64)
            interleave(engine_copy, vg[i][:, q * QUARTER : (q + 1) * QUARTER, :], v_sb[i, q][:])

        def quantize_v(i):
            quantize("v%d" % i, v_codes, v_scales, UNITS[i], flat(vg[i]), HALF)

        def quantize_v_half(i, q):
            key = UNITS[i]
            if q == 0:
                v_codes[key] = keep.tile([P, HALF], U32, name="c_v%d" % i, align_bytes=64)
                v_scales[key] = keep.tile([P, HALF], U8, name="s_v%d" % i, align_bytes=64)
            cols = slice(q * QUARTER, (q + 1) * QUARTER)
            nc.vector.quantize_mx(
                out=v_codes[key][:, cols].bitcast(FP8X4),
                scales=v_scales[key][:, cols],
                in_=vg[i][:, cols, :].rearrange("p n t -> p (n t)"),
            )

        planes, pg, pp = {}, {}, {}

        def widen_psi(g, first=0, last=PACK):
            if first == 0:
                planes[g] = work.tile([P, PACK, C], BF16, name="planes%d" % g, tag="planes", bufs=2)
            for t in range(first, last):
                nc.scalar.activation(
                    out=planes[g][:, t, :],
                    in_=bytes_sb[g][:, t * C : (t + 1) * C].bitcast(FP8),
                    func=COPY,
                    scale=scale_sb[:, g, t : t + 1],
                )

        def group_psi_scalar(g):
            pg[g] = grouped_tile("pg%d" % g)
            for q in range(2):
                cols = slice(q * QUARTER, (q + 1) * QUARTER)
                interleave(nc.scalar.copy, pg[g][:, cols, :], planes[g][:, :, cols])

        def group_psi(g):
            for q in range(2):
                ps = psum.tile([P, QUARTER, PACK], BF16, name="pp%d%d" % (g, q), tag=X_BANKS[q])
                pp[g, q] = ps
                for s in range(2):
                    first = q * QUARTER + s * P
                    nc.tensor.matmul(
                        out=ps[:, s * P : (s + 1) * P, :],
                        lhsT=ident_bf[:],
                        rhs=planes[g][:, :, first : first + P].rearrange("p t c -> p c t"),
                        start=True,
                        stop=True,
                    )

        def copy_psi(g):
            pg[g] = grouped_tile("pg%d" % g)
            for q in range(2):
                nc.scalar.copy(out=pg[g][:, q * QUARTER : (q + 1) * QUARTER, :], in_=pp[g, q][:])

        def quantize_psi(g):
            quantize("psi%d" % g, psi_codes, psi_scales, g, flat(pg[g]), C)

        acc = {}

        def stage2(n, c, cols, bank, groups):
            key = n, c, cols.start
            width = cols.stop - cols.start
            if groups[0] == 0:
                acc[key] = psum.tile([P, width], F32, name="acc%d%d%d" % key, tag=bank)
            for g in groups:
                nc.tensor.matmul_mx(
                    out=acc[key][:],
                    lhsT=psi_codes[g][:, c * P : (c + 1) * P].bitcast(FP8X4),
                    lhsT_scale=psi_scales[g][:, c * P : (c + 1) * P],
                    rhs=v_codes[g, n][:, cols].bitcast(FP8X4),
                    rhs_scale=v_scales[g, n][:, cols],
                    start=(g == 0),
                    stop=(g == 3),
                )

        def store(n, c, cols, engine_copy, tag, bufs):
            key = n, c, cols.start
            width = cols.stop - cols.start
            res = work.tile([P, width], F32, name="res%d%d%d" % key, tag=tag, bufs=bufs)
            engine_copy(out=res[:], in_=acc[key][:])
            first = n * HALF + cols.start
            nc.sync.dma_start(out=out[c * P : (c + 1) * P, first : first + width], in_=res[:])

        alloc_u(0)
        load_u(0, 0, 1)
        load_h(0, 0)
        load_h(1, 0)
        for t in range(1, PACK):
            load_u(0, t, t + 1)
        scale_sb = keep.tile([P, 4, PACK], F32, name="scale_sb")
        nc.sync.dma_start(
            out=scale_sb[:], in_=psi_scale.rearrange("(g p t) o -> p g (t o)", g=4, p=P, t=PACK)
        )
        load_psi(0)
        load_box(0, 0)
        alloc_u(1)
        load_u(1, 0, 2)
        load_u(1, 2, 4)
        load_h(0, 1)
        load_h(1, 1)
        load_box(1, 0)
        alloc_u(2)
        load_u(2, 0, 2)
        load_box(0, 1)
        load_u(2, 2, 4)
        load_psi(1)
        load_box(1, 1)
        alloc_u(3)
        load_u(3, 0, PACK)
        load_box(2, 0)
        load_psi(2)
        load_box(3, 0)
        load_psi(3)

        hg = {}
        hg[0] = grouped_tile("hg00")
        hg[1] = grouped_tile("hg10")

        def group_h_shared(k):
            interleave(nc.vector.tensor_copy, hg[k][:, :H_VECTOR, :], h_raw[k, 0][:, :, :H_VECTOR])
            interleave(nc.scalar.copy, hg[k][:, H_VECTOR:, :], h_raw[k, 0][:, :, H_VECTOR:])

        turn_u(0, X_BANKS[0])
        group_h_shared(0)
        quantize_u_one(0)
        group_h_shared(1)
        turn_u(1, X_BANKS[1])
        quantize("h00", h_codes, h_scales, (0, 0), flat(hg[0]), HALF)
        turn_u(2, X_BANKS[2])
        quantize("h10", h_codes, h_scales, (1, 0), flat(hg[1]), HALF)
        turn_u(3, X_BANKS[3])
        stage1(0, 0)
        quantize_u_one(1)
        stage1(0, 1)
        quantize_u_one(2)
        stage1(0, 2)
        widen_psi(0)
        sub(0, 0)
        quantize_u_one(3)
        stage1(0, 3)
        for j in (4, 5, 6, 7):
            turn_u(j, X_BANKS[j % 4])
        sub(0, 1)
        sub(0, 2)
        sub(0, 3)
        hg[3] = grouped_tile("hg11")
        clamp_lo(0)
        quantize_u_pair(2)
        stage1(1, 0)
        stage1(1, 1)
        clamp_hi(0, 0)
        group_v(0, 0, nc.scalar.copy)
        quantize_u_pair(3)
        stage1(1, 2)
        stage1(1, 3)
        clamp_hi(0, 1)
        group_v(0, 1, nc.scalar.copy)
        hg[2] = grouped_tile("hg01")
        for q in range(2):
            cols = slice(q * QUARTER, (q + 1) * QUARTER)
            interleave(nc.scalar.copy, hg[2][:, cols, :], h_raw[0, 1][:, :, cols])
        interleave(nc.vector.tensor_copy, hg[3][:], h_raw[1, 1][:])

        whole, quarter = slice(0, HALF), (slice(0, QUARTER), slice(QUARTER, HALF))

        def accumulate(n, cols, banks, groups):
            for c in range(4):
                stage2(n, c, cols, banks[c], groups)

        pairs = {1: (4,), 2: (5,), 3: (6, 7)}
        for i in range(1, LAST):
            for k, pair in enumerate(pairs.get(i, ())):
                turn_u(2 * pair, X_BANKS[2 * k])
                turn_u(2 * pair + 1, X_BANKS[2 * k + 1])
            for t in range(PACK):
                sub(i, t)
            if i == 1:
                group_psi_scalar(0)
            if i == 2:
                widen_psi(1)
            if i == 3:
                widen_psi(2, 0, 2)
            if i == 4:
                widen_psi(2, 2, 4)
            if i == 5:
                widen_psi(3)
            if i == 6:
                group_psi_scalar(3)
            if i != 1:
                for t in range(PACK):
                    stage1(i + 1, t)
            if i in (4, 5):
                group_psi({4: 1, 5: 2}[i])
            if i == 6:
                accumulate(0, whole, X_BANKS, (0, 1))
            if i == 1:
                quantize("h11", h_codes, h_scales, (1, 1), flat(hg[3]), HALF)
            else:
                quantize_v(i - 1)
            clamp_lo(i)
            if i == 1:
                quantize_v(0)
                quantize("h01", h_codes, h_scales, (0, 1), flat(hg[2]), HALF)
                for t in range(PACK):
                    stage1(i + 1, t)
            for pair in pairs.get(i, ()):
                quantize_u_pair(pair)
            if i in (2, 5, 6):
                quantize_psi({2: 0, 5: 1, 6: 2}[i])
            if i == 6:
                accumulate(0, whole, X_BANKS, (2,))
            clamp_hi(i, 0)
            group_v(i, 0, nc.scalar.copy)
            clamp_hi(i, 1)
            group_v(i, 1, nc.scalar.copy)
            if i in (4, 5):
                copy_psi({4: 1, 5: 2}[i])
            if i == 1:
                load_box(2, 1)
                load_box(3, 1)

        for t in range(PACK):
            sub(LAST, t)
        quantize_psi(3)
        accumulate(0, whole, X_BANKS, (3,))
        for c in range(4):
            store(0, c, whole, nc.scalar.copy, "res", 4)
        for q in range(2):
            accumulate(1, quarter[q], (G_BANKS, X_BANKS)[q], (0, 1))
        clamp_lo(LAST, quarter[0])
        clamp_lo(LAST, quarter[1])
        quantize_v(LAST - 1)
        for q in range(2):
            accumulate(1, quarter[q], (G_BANKS, X_BANKS)[q], (2,))
        clamp_hi(LAST, 0)
        clamp_hi(LAST, 1)
        vg[LAST] = work.tile([P, HALF, PACK], BF16, name="vg_last", tag="vg", bufs=2, align_bytes=64)
        for q in range(2):
            for s, engine_copy in enumerate((nc.scalar.copy, nc.vector.tensor_copy)):
                part = slice(q * QUARTER + s * P, q * QUARTER + (s + 1) * P)
                interleave(engine_copy, vg[LAST][:, part, :], v_sb[LAST, q][:, :, s * P : (s + 1) * P])
            quantize_v_half(LAST, q)
            for c in range(4):
                stage2(1, c, quarter[q], (G_BANKS, X_BANKS)[q][c], (3,))
        for c in range(4):
            store(1, c, quarter[0], nc.scalar.copy, "rows", 16)
        for c in range(4):
            store(1, c, quarter[1], nc.vector.tensor_copy if c < 3 else nc.scalar.copy, "rows", 16)
